import numpy as np, ml_dtypes
CORES = [25,29,65,69,153,157,193,197]
N = 8
import mx_ref
NC, G = 128, 4
C = np.float32(0.0133)
BF = ml_dtypes.bfloat16
def cut(t, i, w=512):
    return t[:, w * i:w * i + w]
def tile(rs):
    return np.stack(rs, axis=2).reshape(128, -1).astype(BF)
def layer(w, X):
    out = []
    for i in range(G):
        for t in range(len(X)):
            p = mx_ref.matmul(mx_ref.quantize(cut(w, len(X) * i + t)), X[t])
            z = p if t == 0 else z + p
        out.append(z)
    return out
def act(Z):
    return [np.maximum(z, 0) * C for z in Z]
def setup_inputs(rng):
    def f(*shape):
        return mx_ref.flush((rng.standard_normal(shape, dtype=np.float32) * np.exp2(rng.integers(-2, 3, shape[:-1] + (1,)))).astype(BF))
    return {"s": f(N, 128, 4 * NC), "x": f(N, 128, 4 * NC), "w": f(N, 128, 2 * G * 512), "v": f(N, 128, 512)}
def setup_inputs_blocks(rng):
    d = setup_inputs(rng)
    for k in ("s", "x", "v"): d[k] = mx_ref.spread(d[k], rng, 4)
    for k in ("w",): d[k] = mx_ref.spread(d[k], rng, 1)
    return d
def setup_inputs_wide(rng):
    d = setup_inputs(rng)
    for k in ("s", "x", "v"): d[k] = mx_ref.flush((d[k].astype(np.float32) * np.exp2(rng.integers(-6, 7, (N, 1, 1))).astype(np.float32)).astype(BF))
    return d
def setup_inputs_zeros(rng):
    d = setup_inputs(rng); v = d["x"].reshape(N, 128, -1, 4).copy()
    v[np.broadcast_to((rng.random((N, 1, v.shape[2], 1)) < 0.33), v.shape)] = 0
    d["x"] = v.reshape(d["x"].shape)
    return d
def reference(s, x, w, v):
    q = mx_ref.quantize(s[0])
    y = np.zeros((N, 128, NC), np.float32)
    for r in range(N):
        q = mx_ref.quantize(tile(act(layer(w[r], [q, mx_ref.quantize(x[r])]))))
        y[r] = mx_ref.matmul(mx_ref.quantize(v[r]), q)
    return {"y": y}

@@ -1,0 +1,182 @@
+import numpy as np
+from concourse.mybir import dt, AluOpType, ActivationFunctionType
+
+NC, G = 128, 4
+TW = 4 * NC
+CF = float(np.float32(0.0133))
+SIM_CORES = 256
+
+SCRATCH = {
+    "st": ("sbuf", [128, TW], "bfloat16"),
+    "xt": ("sbuf", [128, TW], "bfloat16"),
+    "wt": ("sbuf", [128, 2 * G * TW], "bfloat16"),
+    "vt": ("sbuf", [128, TW], "bfloat16"),
+    "sq": ("sbuf", [128, NC], "float8_e4m3fn_x4"), "ss": ("sbuf", [128, NC], "uint8"),
+    "xq": ("sbuf", [128, NC], "float8_e4m3fn_x4"), "xs": ("sbuf", [128, NC], "uint8"),
+    "wq": ("sbuf", [128, 2 * G * NC], "float8_e4m3fn_x4"), "ws": ("sbuf", [128, 2 * G * NC], "uint8"),
+    "vq": ("sbuf", [128, NC], "float8_e4m3fn_x4"), "vs": ("sbuf", [128, NC], "uint8"),
+    "qin": ("sbuf", [128, NC], "float8_e4m3fn_x4"), "qins": ("sbuf", [128, NC], "uint8"),
+    "h": ("sbuf", [128, TW], "bfloat16"),
+    "qo": ("sbuf", [128, NC], "float8_e4m3fn_x4"), "qos": ("sbuf", [128, NC], "uint8"),
+    "yb": ("sbuf", [128, NC], "float32"),
+    "z": ("psum", [128, 512 * G], "float32"),
+    "yp": ("psum", [128, 512], "float32"),
+}
+SEMAPHORES = (["ld_s", "ld_x", "ld_v"] + ["ld_w%d" % i for i in range(G)]
+              + ["qz_s", "qz_x", "qz_v", "qz_q"] + ["qz_w%d" % k for k in range(2 * G)]
+              + ["mm%d" % i for i in range(G)] + ["mm_y", "act", "ycp", "stored", "arr", "sent"])
+
+
+def _plan(cores, topo):
+    hops = []
+    for r in range(len(cores) - 1):
+        src, dst = cores[r], cores[r + 1]
+        if topo.may_write(src, dst):
+            hops.append((src, dst, None, None))
+            continue
+        near = [c for c in range(SIM_CORES) if c not in cores and topo.host(c) == topo.host(src)
+                and topo.chip(c) == topo.chip(src) and topo.may_write(src, c) and topo.may_write(c, dst)]
+        near.sort(key=lambda c: (topo.die(c) != topo.die(src), c))
+        hops.append((src, dst, near[0], near[1]))
+    return hops
+
+
+def _engines(mask):
+    return [b for b in range(mask.bit_length()) if (mask >> b) & 1]
+
+
+def _bits(engines):
+    m = 0
+    for b in engines:
+        m |= 1 << b
+    return m
+
+
+def _write(g, T, topo, src, dst, out_ap, in_ap, engines):
+    rid, pid = topo.addr(dst, src)
+    g.remote_dma(out_ap, in_ap, T.sem.arr, T.sem.sent, pid, rid, _bits(engines))
+    return len(engines)
+
+
+def _halves(topo, src, dst_c, dst_s):
+    return _engines(topo.mask(src, dst_c))[0::2], _engines(topo.mask(src, dst_s))[1::2]
+
+
+def rank_program(g, core, T, topo):
+    cores = list(T.cores)
+    hops = _plan(cores, topo)
+    rank = T.rank_of(core)
+    s = T.sem
+
+    if rank is None:
+        for src, dst, hc, hs in hops:
+            if core not in (hc, hs):
+                continue
+            ec, es = _halves(topo, src, hc, hs)
+            out = _engines(topo.mask(core, dst))
+            if core == hc:
+                g.wait_ge(s.arr, len(ec))
+                n = _write(g, T, topo, core, dst, T.qin[:].bitcast(dt.uint8), T.qin[:].bitcast(dt.uint8), out)
+            else:
+                g.wait_ge(s.arr, len(es))
+                n = _write(g, T, topo, core, dst, T.qins[:], T.qins[:], out)
+            g.wait_ge(s.sent, n)
+        return
+
+    first, last = rank == 0, rank == len(cores) - 1
+    TE, V, SC, SY = g.tensor, g.vector, g.scalar, g.sync
+
+    loads = []
+    if first:
+        loads.append((T.st[:], T.s[:], s.ld_s))
+    loads.append((T.xt[:], T.x[:], s.ld_x))
+    for i in range(G):
+        loads.append((T.wt[:, 2 * TW * i:2 * TW * (i + 1)], T.w[:, 2 * TW * i:2 * TW * (i + 1)], s["ld_w%d" % i]))
+    loads.append((T.vt[:], T.v[:], s.ld_v))
+    for k, (o, i_, sem) in enumerate(loads):
+        (SY if k % 2 == 0 else SC).dma_start(o, i_).then_inc(sem, 16)
+
+    def wcol(k):
+        return slice(NC * k, NC * (k + 1))
+
+    def zbank(i):
+        return T.z[:, 512 * i:512 * i + NC]
+
+    def quant_w(i):
+        V.wait_ge(s["ld_w%d" % i], 16)
+        for k in (2 * i, 2 * i + 1):
+            V.quantize_mx(T.wq[:, wcol(k)], T.ws[:, wcol(k)], T.wt[:, TW * k:TW * (k + 1)]).then_inc(s["qz_w%d" % k], 1)
+
+    def quant_v():
+        V.wait_ge(s.ld_v, 16)
+        V.quantize_mx(T.vq[:], T.vs[:], T.vt[:]).then_inc(s.qz_v, 1)
+
+    def act_v(i):
+        V.wait_ge(s["mm%d" % i], 1)
+        V.tensor_scalar(T.h[:, i:TW:4], zbank(i), 0.0, CF, AluOpType.max, AluOpType.mult).then_inc(s.act, 1)
+
+    if first:
+        V.wait_ge(s.ld_s, 16)
+        V.quantize_mx(T.sq[:], T.ss[:], T.st[:]).then_inc(s.qz_s, 1)
+    V.wait_ge(s.ld_x, 16)
+    V.quantize_mx(T.xq[:], T.xs[:], T.xt[:]).then_inc(s.qz_x, 1)
+    if first:
+        quant_w(0); quant_w(1); act_v(1); quant_w(2); quant_w(3); act_v(3)
+    else:
+        for i in range(G):
+            quant_w(i)
+        quant_v()
+        act_v(1); act_v(3)
+    V.wait_ge(s.act, G)
+    V.quantize_mx(T.qo[:], T.qos[:], T.h[:]).then_inc(s.qz_q, 1)
+    if first:
+        quant_v()
+
+    for i in (0, 2):
+        SC.wait_ge(s["mm%d" % i], 1)
+        SC.activation(T.h[:, i:TW:4], zbank(i), ActivationFunctionType.Relu, scale=CF).then_inc(s.act, 1)
+
+    def mm(i, t, rhs, rhs_s, start, stop):
+        k = 2 * i + t
+        return TE.matmul_mx(zbank(i), T.wq[:, wcol(k)], T.ws[:, wcol(k)], rhs, rhs_s, start, stop)
+
+    TE.wait_ge(s.qz_x, 1)
+    if first:
+        TE.wait_ge(s.qz_s, 1)
+        for i in range(G):
+            TE.wait_ge(s["qz_w%d" % (2 * i)], 1)
+            mm(i, 0, T.sq[:], T.ss[:], True, False)
+            TE.wait_ge(s["qz_w%d" % (2 * i + 1)], 1)
+            mm(i, 1, T.xq[:], T.xs[:], False, True).then_inc(s["mm%d" % i], 1)
+    else:
+        for i in range(G):
+            TE.wait_ge(s["qz_w%d" % (2 * i)], 1)
+            TE.wait_ge(s["qz_w%d" % (2 * i + 1)], 1)
+            mm(i, 1, T.xq[:], T.xs[:], True, False)
+        src, _, hc, hs = hops[rank - 1]
+        if hc is None:
+            ec, es = _halves(topo, src, core, core)
+            n_in = len(ec) + len(es)
+        else:
+            n_in = len(_engines(topo.mask(hc, core))) + len(_engines(topo.mask(hs, core)))
+        TE.wait_ge(s.arr, n_in)
+        for i in range(G):
+            mm(i, 0, T.qin[:], T.qins[:], False, True).then_inc(s["mm%d" % i], 1)
+    TE.wait_ge(s.qz_v, 1)
+    TE.wait_ge(s.qz_q, 1)
+    TE.matmul_mx(T.yp[:, 0:NC], T.vq[:], T.vs[:], T.qo[:], T.qos[:], True, True).then_inc(s.mm_y, 1)
+
+    if not last:
+        _, dst, hc, hs = hops[rank]
+        dc, ds = (dst, dst) if hc is None else (hc, hs)
+        ec, es = _halves(topo, core, dc, ds)
+        g.wait_ge(s.qz_q, 1)
+        n = _write(g, T, topo, core, dc, T.qin[:].bitcast(dt.uint8), T.qo[:].bitcast(dt.uint8), ec)
+        n += _write(g, T, topo, core, ds, T.qins[:], T.qos[:], es)
+        g.wait_ge(s.sent, n)
+
+    SC.wait_ge(s.mm_y, 1)
+    SC.activation(T.yb[:], T.yp[:, 0:NC], ActivationFunctionType.Copy).then_inc(s.ycp, 1)
+    SY.wait_ge(s.ycp, 1)
+    SY.dma_start(T.y[:], T.yb[:]).then_inc(s.stored, 16)
+    SY.wait_ge(s.stored, 16)

@@ -3,6 +3,7 @@ from concourse.mybir import dt, AluOpType, ActivationFunctionType
 
 NC, G = 128, 4
 TW = 4 * NC
+NT = 1 + 2 * G
 CF = float(np.float32(0.0133))
 SIM_CORES = 256
 
@@ -12,10 +13,11 @@ SCRATCH = {
     "wt": ("sbuf", [128, 2 * G * TW], "bfloat16"),
     "vt": ("sbuf", [128, TW], "bfloat16"),
     "sq": ("sbuf", [128, NC], "float8_e4m3fn_x4"), "ss": ("sbuf", [128, NC], "uint8"),
-    "xq": ("sbuf", [128, NC], "float8_e4m3fn_x4"), "xs": ("sbuf", [128, NC], "uint8"),
-    "wq": ("sbuf", [128, 2 * G * NC], "float8_e4m3fn_x4"), "ws": ("sbuf", [128, 2 * G * NC], "uint8"),
+    "bq": ("sbuf", [128, NT * NC], "float8_e4m3fn_x4"), "bs": ("sbuf", [128, NT * NC], "uint8"),
+    "rq": ("sbuf", [128, NT * NC], "float8_e4m3fn_x4"), "rs": ("sbuf", [128, NT * NC], "uint8"),
     "vq": ("sbuf", [128, NC], "float8_e4m3fn_x4"), "vs": ("sbuf", [128, NC], "uint8"),
     "qin": ("sbuf", [128, NC], "float8_e4m3fn_x4"), "qins": ("sbuf", [128, NC], "uint8"),
+    "qy": ("sbuf", [128, NC], "float8_e4m3fn_x4"), "qys": ("sbuf", [128, NC], "uint8"),
     "h": ("sbuf", [128, TW], "bfloat16"),
     "qo": ("sbuf", [128, NC], "float8_e4m3fn_x4"), "qos": ("sbuf", [128, NC], "uint8"),
     "yb": ("sbuf", [128, NC], "float32"),
@@ -24,21 +26,74 @@ SCRATCH = {
 }
 SEMAPHORES = (["ld_s", "ld_x", "ld_v"] + ["ld_w%d" % i for i in range(G)]
               + ["qz_s", "qz_x", "qz_v", "qz_q"] + ["qz_w%d" % k for k in range(2 * G)]
-              + ["mm%d" % i for i in range(G)] + ["mm_y", "act", "ycp", "stored", "arr", "sent"])
+              + ["mm%d" % i for i in range(G)] + ["mm_y", "act", "ycp", "stored", "arr", "yarr", "sent"]
+              + ["hb%d" % i for i in range(G)] + ["rb%d" % i for i in range(G)])
+
+_CACHE = {}
+
+
+def _perms(items):
+    if not items:
+        return [()]
+    out = []
+    for i, a in enumerate(items):
+        for rest in _perms(items[:i] + items[i + 1:]):
+            out.append((a,) + rest)
+    return out
+
+
+def _same_chip(topo, a, b):
+    return topo.host(a) == topo.host(b) and topo.chip(a) == topo.chip(b)
+
+
+def _pair(cores, topo, src, dst):
+    if topo.may_write(src, dst):
+        return None
+    near = [c for c in range(SIM_CORES) if c not in cores and _same_chip(topo, c, src)
+            and topo.may_write(src, c) and topo.may_write(c, dst)]
+    near.sort(key=lambda c: (topo.die(c) != topo.die(src), c))
+    return near[0], near[1]
 
 
 def _plan(cores, topo):
-    hops = []
-    for r in range(len(cores) - 1):
-        src, dst = cores[r], cores[r + 1]
-        if topo.may_write(src, dst):
-            hops.append((src, dst, None, None))
-            continue
-        near = [c for c in range(SIM_CORES) if c not in cores and topo.host(c) == topo.host(src)
-                and topo.chip(c) == topo.chip(src) and topo.may_write(src, c) and topo.may_write(c, dst)]
-        near.sort(key=lambda c: (topo.die(c) != topo.die(src), c))
-        hops.append((src, dst, near[0], near[1]))
-    return hops
+    if "plan" in _CACHE:
+        return _CACHE["plan"]
+    n = len(cores)
+    best = None
+    for mid in _perms(tuple(range(1, n - 1))):
+        h = (0,) + mid + (n - 1,)
+        key = (sum(not topo.may_write(cores[h[l]], cores[h[l + 1]]) for l in range(n - 1)),
+               sum(h[l] != l for l in range(n)),
+               sum(h[l] != l and h[l + 1] != l for l in range(n - 1)),
+               sum(topo.die(cores[h[l]]) != topo.die(cores[h[l + 1]]) for l in range(n - 1)), h)
+        if best is None or key < best:
+            best = key
+    host = best[-1]
+    qdst = []
+    for l in range(n):
+        d = []
+        if l < n - 1:
+            d.append((cores[host[l + 1]], "c"))
+            if host[l] != l and host[l + 1] != l:
+                d.append((cores[l], "y"))
+        qdst.append(d)
+    jobs = {}
+    for l in range(n):
+        if host[l] != l:
+            src, dst = cores[l], cores[host[l]]
+            hp = _pair(cores, topo, src, dst)
+            if hp:
+                for j in range(G):
+                    jobs.setdefault(hp[j % 2], []).append(("b", j, src, dst))
+    for l in range(n):
+        src = cores[host[l]]
+        via = [(d, k) for d, k in qdst[l] if not topo.may_write(src, d)]
+        if via:
+            hp = _pair(cores, topo, src, via[0][0])
+            jobs.setdefault(hp[0], []).append(("q", 0, src, via))
+            jobs.setdefault(hp[1], []).append(("q", 1, src, via))
+    _CACHE["plan"] = (host, qdst, jobs)
+    return _CACHE["plan"]
 
 
 def _engines(mask):
@@ -52,39 +107,68 @@ def _bits(engines):
     return m
 
 
-def _write(g, T, topo, src, dst, out_ap, in_ap, engines):
-    rid, pid = topo.addr(dst, src)
-    g.remote_dma(out_ap, in_ap, T.sem.arr, T.sem.sent, pid, rid, _bits(engines))
-    return len(engines)
+def _q_engines(topo, src, dst_c, dst_s):
+    mc, ms = _engines(topo.mask(src, dst_c)), _engines(topo.mask(src, dst_s))
+    if _same_chip(topo, src, dst_c):
+        return mc[0::2], ms[1::2]
+    return mc, ms
 
 
-def _halves(topo, src, dst_c, dst_s):
-    return _engines(topo.mask(src, dst_c))[0::2], _engines(topo.mask(src, dst_s))[1::2]
+def _q_count(cores, topo, src, dst):
+    hp = _pair(cores, topo, src, dst)
+    if hp is None:
+        ec, es = _q_engines(topo, src, dst, dst)
+        return len(ec) + len(es)
+    return len(_engines(topo.mask(hp[0], dst))) + len(_engines(topo.mask(hp[1], dst)))
+
+
+def _piece(j):
+    return slice(0 if j == 0 else NC * (1 + 2 * j), NC * (3 + 2 * j))
 
 
 def rank_program(g, core, T, topo):
     cores = list(T.cores)
-    hops = _plan(cores, topo)
+    host, qdst, jobs = _plan(cores, topo)
     rank = T.rank_of(core)
     s = T.sem
+    n_sent = [0]
+
+    def write(dst, out_ap, in_ap, sem, engines):
+        rid, pid = topo.addr(dst, core)
+        g.remote_dma(out_ap, in_ap, sem, s.sent, pid, rid, _bits(engines))
+        n_sent[0] += len(engines)
+
+    def land(kind):
+        return (T.qin, T.qins, s.arr) if kind == "c" else (T.qy, T.qys, s.yarr)
 
     if rank is None:
-        for src, dst, hc, hs in hops:
-            if core not in (hc, hs):
-                continue
-            ec, es = _halves(topo, src, hc, hs)
-            out = _engines(topo.mask(core, dst))
-            if core == hc:
-                g.wait_ge(s.arr, len(ec))
-                n = _write(g, T, topo, core, dst, T.qin[:].bitcast(dt.uint8), T.qin[:].bitcast(dt.uint8), out)
+        for what, j, src, to in jobs.get(core, []):
+            if what == "b":
+                c = _piece(j)
+                g.wait_ge(s["hb%d" % j], 2 * len(_engines(topo.mask(src, core))))
+                e = _engines(topo.mask(core, to))
+                write(to, T.rq[:, c].bitcast(dt.uint8), T.rq[:, c].bitcast(dt.uint8), s["rb%d" % j], e)
+                write(to, T.rs[:, c], T.rs[:, c], s["rb%d" % j], e)
             else:
-                g.wait_ge(s.arr, len(es))
-                n = _write(g, T, topo, core, dst, T.qins[:], T.qins[:], out)
-            g.wait_ge(s.sent, n)
+                hp = _pair(cores, topo, src, to[0][0])
+                g.wait_ge(s.arr, len(_q_engines(topo, src, hp[0], hp[1])[j]))
+                for dst, kind in to:
+                    oc, os_, sem = land(kind)
+                    e = _engines(topo.mask(core, dst))
+                    if j == 0:
+                        write(dst, oc[:].bitcast(dt.uint8), T.qin[:].bitcast(dt.uint8), sem, e)
+                    else:
+                        write(dst, os_[:], T.qins[:], sem, e)
+        if n_sent[0]:
+            g.wait_ge(s.sent, n_sent[0])
         return
 
-    first, last = rank == 0, rank == len(cores) - 1
+    n = len(cores)
+    lay = host.index(rank)
+    home = lay == rank
+    first = lay == 0
     TE, V, SC, SY = g.tensor, g.vector, g.scalar, g.sync
+    Wq, Ws = (T.bq, T.bs) if home else (T.rq, T.rs)
 
     loads = []
     if first:
@@ -97,7 +181,7 @@ def rank_program(g, core, T, topo):
         (SY if k % 2 == 0 else SC).dma_start(o, i_).then_inc(sem, 16)
 
     def wcol(k):
-        return slice(NC * k, NC * (k + 1))
+        return slice(NC * (k + 1), NC * (k + 2))
 
     def zbank(i):
         return T.z[:, 512 * i:512 * i + NC]
@@ -105,7 +189,7 @@ def rank_program(g, core, T, topo):
     def quant_w(i):
         V.wait_ge(s["ld_w%d" % i], 16)
         for k in (2 * i, 2 * i + 1):
-            V.quantize_mx(T.wq[:, wcol(k)], T.ws[:, wcol(k)], T.wt[:, TW * k:TW * (k + 1)]).then_inc(s["qz_w%d" % k], 1)
+            V.quantize_mx(T.bq[:, wcol(k)], T.bs[:, wcol(k)], T.wt[:, TW * k:TW * (k + 1)]).then_inc(s["qz_w%d" % k], 1)
 
     def quant_v():
         V.wait_ge(s.ld_v, 16)
@@ -119,7 +203,7 @@ def rank_program(g, core, T, topo):
         V.wait_ge(s.ld_s, 16)
         V.quantize_mx(T.sq[:], T.ss[:], T.st[:]).then_inc(s.qz_s, 1)
     V.wait_ge(s.ld_x, 16)
-    V.quantize_mx(T.xq[:], T.xs[:], T.xt[:]).then_inc(s.qz_x, 1)
+    V.quantize_mx(T.bq[:, 0:NC], T.bs[:, 0:NC], T.xt[:]).then_inc(s.qz_x, 1)
     if first:
         quant_w(0); quant_w(1); act_v(1); quant_w(2); quant_w(3); act_v(3)
     else:
@@ -138,42 +222,72 @@ def rank_program(g, core, T, topo):
 
     def mm(i, t, rhs, rhs_s, start, stop):
         k = 2 * i + t
-        return TE.matmul_mx(zbank(i), T.wq[:, wcol(k)], T.ws[:, wcol(k)], rhs, rhs_s, start, stop)
+        return TE.matmul_mx(zbank(i), Wq[:, wcol(k)], Ws[:, wcol(k)], rhs, rhs_s, start, stop)
 
-    TE.wait_ge(s.qz_x, 1)
     if first:
+        TE.wait_ge(s.qz_x, 1)
         TE.wait_ge(s.qz_s, 1)
         for i in range(G):
             TE.wait_ge(s["qz_w%d" % (2 * i)], 1)
             mm(i, 0, T.sq[:], T.ss[:], True, False)
             TE.wait_ge(s["qz_w%d" % (2 * i + 1)], 1)
-            mm(i, 1, T.xq[:], T.xs[:], False, True).then_inc(s["mm%d" % i], 1)
+            mm(i, 1, Wq[:, 0:NC], Ws[:, 0:NC], False, True).then_inc(s["mm%d" % i], 1)
     else:
-        for i in range(G):
-            TE.wait_ge(s["qz_w%d" % (2 * i)], 1)
-            TE.wait_ge(s["qz_w%d" % (2 * i + 1)], 1)
-            mm(i, 1, T.xq[:], T.xs[:], True, False)
-        src, _, hc, hs = hops[rank - 1]
-        if hc is None:
-            ec, es = _halves(topo, src, core, core)
-            n_in = len(ec) + len(es)
+        if home:
+            TE.wait_ge(s.qz_x, 1)
         else:
-            n_in = len(_engines(topo.mask(hc, core))) + len(_engines(topo.mask(hs, core)))
-        TE.wait_ge(s.arr, n_in)
+            hp = _pair(cores, topo, cores[lay], core)
+        for i in range(G):
+            if home:
+                TE.wait_ge(s["qz_w%d" % (2 * i)], 1)
+                TE.wait_ge(s["qz_w%d" % (2 * i + 1)], 1)
+            else:
+                TE.wait_ge(s["rb%d" % i], 2 * len(_engines(topo.mask(hp[i % 2] if hp else cores[lay], core))))
+            mm(i, 1, Wq[:, 0:NC], Ws[:, 0:NC], True, False)
+        TE.wait_ge(s.arr, _q_count(cores, topo, cores[host[lay - 1]], core))
         for i in range(G):
             mm(i, 0, T.qin[:], T.qins[:], False, True).then_inc(s["mm%d" % i], 1)
     TE.wait_ge(s.qz_v, 1)
-    TE.wait_ge(s.qz_q, 1)
-    TE.matmul_mx(T.yp[:, 0:NC], T.vq[:], T.vs[:], T.qo[:], T.qos[:], True, True).then_inc(s.mm_y, 1)
+    if home:
+        TE.wait_ge(s.qz_q, 1)
+        yq, ys = T.qo, T.qos
+    elif lay == rank + 1:
+        yq, ys = T.qin, T.qins
+    else:
+        TE.wait_ge(s.yarr, _q_count(cores, topo, cores[host[rank]], core))
+        yq, ys = T.qy, T.qys
+    TE.matmul_mx(T.yp[:, 0:NC], T.vq[:], T.vs[:], yq[:], ys[:], True, True).then_inc(s.mm_y, 1)
 
-    if not last:
-        _, dst, hc, hs = hops[rank]
-        dc, ds = (dst, dst) if hc is None else (hc, hs)
-        ec, es = _halves(topo, core, dc, ds)
+    if not home:
+        to = cores[host[rank]]
+        hp = _pair(cores, topo, core, to)
+        g.wait_ge(s.qz_x, 1)
+        for j in range(G):
+            g.wait_ge(s["qz_w%d" % (2 * j)], 1)
+            g.wait_ge(s["qz_w%d" % (2 * j + 1)], 1)
+            c = _piece(j)
+            d, sem = (hp[j % 2], s["hb%d" % j]) if hp else (to, s["rb%d" % j])
+            e = _engines(topo.mask(core, d))
+            write(d, T.rq[:, c].bitcast(dt.uint8), T.bq[:, c].bitcast(dt.uint8), sem, e)
+            write(d, T.rs[:, c], T.bs[:, c], sem, e)
+
+    if qdst[lay]:
         g.wait_ge(s.qz_q, 1)
-        n = _write(g, T, topo, core, dc, T.qin[:].bitcast(dt.uint8), T.qo[:].bitcast(dt.uint8), ec)
-        n += _write(g, T, topo, core, ds, T.qins[:], T.qos[:], es)
-        g.wait_ge(s.sent, n)
+        handed = False
+        for dst, kind in qdst[lay]:
+            hp = _pair(cores, topo, core, dst)
+            if hp is None:
+                oc, os_, sem = land(kind)
+                ec, es = _q_engines(topo, core, dst, dst)
+                write(dst, oc[:].bitcast(dt.uint8), T.qo[:].bitcast(dt.uint8), sem, ec)
+                write(dst, os_[:], T.qos[:], sem, es)
+            elif not handed:
+                ec, es = _q_engines(topo, core, hp[0], hp[1])
+                write(hp[0], T.qin[:].bitcast(dt.uint8), T.qo[:].bitcast(dt.uint8), s.arr, ec)
+                write(hp[1], T.qins[:], T.qos[:], s.arr, es)
+                handed = True
+    if n_sent[0]:
+        g.wait_ge(s.sent, n_sent[0])
 
     SC.wait_ge(s.mm_y, 1)
     SC.activation(T.yb[:], T.yp[:, 0:NC], ActivationFunctionType.Copy).then_inc(s.ycp, 1)

@@ -26,7 +26,7 @@ SCRATCH = {
 }
 SEMAPHORES = (["ld_s", "ld_x", "ld_v"] + ["ld_w%d" % i for i in range(G)]
               + ["qz_s", "qz_x", "qz_v", "qz_q"] + ["qz_w%d" % k for k in range(2 * G)]
-              + ["mm%d" % i for i in range(G)] + ["mm_y", "act", "ycp", "stored", "arr", "yarr", "sent"]
+              + ["mm%d" % i for i in range(G)] + ["mm_y", "act", "ycp", "stored", "arr", "yarr", "sent", "psent"]
               + ["hb%d" % i for i in range(G)] + ["rb%d" % i for i in range(G)])
 
 _CACHE = {}
@@ -55,6 +55,20 @@ def _pair(cores, topo, src, dst):
     return near[0], near[1]
 
 
+def _ways(cores, topo, src, dst):
+    key = ("ways", src, dst)
+    if key not in _CACHE:
+        near = _pair(cores, topo, src, dst)
+        if near is None:
+            _CACHE[key] = None
+        else:
+            far = [c for c in range(SIM_CORES) if c not in cores and topo.mates(c, dst)
+                   and topo.may_write(src, c) and topo.may_write(c, dst)]
+            far.sort(key=lambda c: (topo.die(c) != topo.die(src), c))
+            _CACHE[key] = tuple((far if j % 2 == 0 else near)[(j // 2) % 2] for j in range(G))
+    return _CACHE[key]
+
+
 def _plan(cores, topo):
     if "plan" in _CACHE:
         return _CACHE["plan"]
@@ -81,10 +95,10 @@ def _plan(cores, topo):
     for l in range(n):
         if host[l] != l:
             src, dst = cores[l], cores[host[l]]
-            hp = _pair(cores, topo, src, dst)
-            if hp:
+            via = _ways(cores, topo, src, dst)
+            if via:
                 for j in range(G):
-                    jobs.setdefault(hp[j % 2], []).append(("b", j, src, dst))
+                    jobs.setdefault(via[j], []).append(("b", j, src, dst))
     for l in range(n):
         src = cores[host[l]]
         via = [(d, k) for d, k in qdst[l] if not topo.may_write(src, d)]
@@ -107,17 +121,34 @@ def _bits(engines):
     return m
 
 
-def _q_engines(topo, src, dst_c, dst_s):
+def _b_engines(cores, topo, src, dst, j):
+    via = _ways(cores, topo, src, dst)
+    if via is None:
+        return _engines(topo.mask(src, dst))
+    e = _engines(topo.mask(src, via[j]))
+    if _same_chip(topo, src, via[j]):
+        away = [b for c in via if not _same_chip(topo, src, c) for b in _engines(topo.mask(src, c))]
+        rest = [b for b in e if b not in away]
+        return rest or e
+    return e
+
+
+def _q_engines(topo, src, dst_c, dst_s, sent_before):
     mc, ms = _engines(topo.mask(src, dst_c)), _engines(topo.mask(src, dst_s))
-    if _same_chip(topo, src, dst_c):
+    if _same_chip(topo, src, dst_c) and not sent_before:
         return mc[0::2], ms[1::2]
     return mc, ms
 
 
-def _q_count(cores, topo, src, dst):
+def _away(cores, host, c):
+    r = cores.index(c)
+    return host[r] != r
+
+
+def _q_count(cores, topo, host, src, dst):
     hp = _pair(cores, topo, src, dst)
     if hp is None:
-        ec, es = _q_engines(topo, src, dst, dst)
+        ec, es = _q_engines(topo, src, dst, dst, _away(cores, host, src))
         return len(ec) + len(es)
     return len(_engines(topo.mask(hp[0], dst))) + len(_engines(topo.mask(hp[1], dst)))
 
@@ -131,12 +162,12 @@ def rank_program(g, core, T, topo):
     host, qdst, jobs = _plan(cores, topo)
     rank = T.rank_of(core)
     s = T.sem
-    n_sent = [0]
+    left = {"sent": 0, "psent": 0}
 
-    def write(dst, out_ap, in_ap, sem, engines):
+    def write(dst, out_ap, in_ap, sem, engines, lsem="sent"):
         rid, pid = topo.addr(dst, core)
-        g.remote_dma(out_ap, in_ap, sem, s.sent, pid, rid, _bits(engines))
-        n_sent[0] += len(engines)
+        g.remote_dma(out_ap, in_ap, sem, s[lsem], pid, rid, _bits(engines))
+        left[lsem] += len(engines)
 
     def land(kind):
         return (T.qin, T.qins, s.arr) if kind == "c" else (T.qy, T.qys, s.yarr)
@@ -145,13 +176,13 @@ def rank_program(g, core, T, topo):
         for what, j, src, to in jobs.get(core, []):
             if what == "b":
                 c = _piece(j)
-                g.wait_ge(s["hb%d" % j], 2 * len(_engines(topo.mask(src, core))))
+                g.wait_ge(s["hb%d" % j], 2 * len(_b_engines(cores, topo, src, to, j)))
                 e = _engines(topo.mask(core, to))
                 write(to, T.rq[:, c].bitcast(dt.uint8), T.rq[:, c].bitcast(dt.uint8), s["rb%d" % j], e)
                 write(to, T.rs[:, c], T.rs[:, c], s["rb%d" % j], e)
             else:
                 hp = _pair(cores, topo, src, to[0][0])
-                g.wait_ge(s.arr, len(_q_engines(topo, src, hp[0], hp[1])[j]))
+                g.wait_ge(s.arr, len(_q_engines(topo, src, hp[0], hp[1], _away(cores, host, src))[j]))
                 for dst, kind in to:
                     oc, os_, sem = land(kind)
                     e = _engines(topo.mask(core, dst))
@@ -159,24 +190,28 @@ def rank_program(g, core, T, topo):
                         write(dst, oc[:].bitcast(dt.uint8), T.qin[:].bitcast(dt.uint8), sem, e)
                     else:
                         write(dst, os_[:], T.qins[:], sem, e)
-        if n_sent[0]:
-            g.wait_ge(s.sent, n_sent[0])
+        if left["sent"]:
+            g.wait_ge(s.sent, left["sent"])
         return
 
-    n = len(cores)
     lay = host.index(rank)
     home = lay == rank
     first = lay == 0
     TE, V, SC, SY = g.tensor, g.vector, g.scalar, g.sync
     Wq, Ws = (T.bq, T.bs) if home else (T.rq, T.rs)
 
+    if first:
+        cuts = ((0, G), (G, 2 * G - 1), (2 * G - 1, 2 * G))
+    else:
+        cuts = tuple((2 * i, 2 * i + 2) for i in range(G))
     loads = []
     if first:
         loads.append((T.st[:], T.s[:], s.ld_s))
     loads.append((T.xt[:], T.x[:], s.ld_x))
-    for i in range(G):
-        loads.append((T.wt[:, 2 * TW * i:2 * TW * (i + 1)], T.w[:, 2 * TW * i:2 * TW * (i + 1)], s["ld_w%d" % i]))
-    loads.append((T.vt[:], T.v[:], s.ld_v))
+    for p, (a, b) in enumerate(cuts):
+        loads.append((T.wt[:, TW * a:TW * b], T.w[:, TW * a:TW * b], s["ld_w%d" % p]))
+    if home:
+        loads.append((T.vt[:], T.v[:], s.ld_v))
     for k, (o, i_, sem) in enumerate(loads):
         (SY if k % 2 == 0 else SC).dma_start(o, i_).then_inc(sem, 16)
 
@@ -186,39 +221,49 @@ def rank_program(g, core, T, topo):
     def zbank(i):
         return T.z[:, 512 * i:512 * i + NC]
 
-    def quant_w(i):
-        V.wait_ge(s["ld_w%d" % i], 16)
-        for k in (2 * i, 2 * i + 1):
-            V.quantize_mx(T.bq[:, wcol(k)], T.bs[:, wcol(k)], T.wt[:, TW * k:TW * (k + 1)]).then_inc(s["qz_w%d" % k], 1)
+    if not home:
+        to = cores[host[rank]]
+        via = _ways(cores, topo, core, to)
+        g.wait_ge(s.qz_x, 1)
+        for j in range(G):
+            g.wait_ge(s["qz_w%d" % (2 * j)], 1)
+            g.wait_ge(s["qz_w%d" % (2 * j + 1)], 1)
+            c = _piece(j)
+            d, sem = (via[j], s["hb%d" % j]) if via else (to, s["rb%d" % j])
+            e = _b_engines(cores, topo, core, to, j)
+            write(d, T.rq[:, c].bitcast(dt.uint8), T.bq[:, c].bitcast(dt.uint8), sem, e, "psent")
+            write(d, T.rs[:, c], T.bs[:, c], sem, e, "psent")
+        SY.wait_ge(s.psent, left["psent"])
+        SY.dma_start(T.vt[:], T.v[:]).then_inc(s.ld_v, 16)
 
     def quant_v():
         V.wait_ge(s.ld_v, 16)
         V.quantize_mx(T.vq[:], T.vs[:], T.vt[:]).then_inc(s.qz_v, 1)
-
-    def act_v(i):
-        V.wait_ge(s["mm%d" % i], 1)
-        V.tensor_scalar(T.h[:, i:TW:4], zbank(i), 0.0, CF, AluOpType.max, AluOpType.mult).then_inc(s.act, 1)
 
     if first:
         V.wait_ge(s.ld_s, 16)
         V.quantize_mx(T.sq[:], T.ss[:], T.st[:]).then_inc(s.qz_s, 1)
     V.wait_ge(s.ld_x, 16)
     V.quantize_mx(T.bq[:, 0:NC], T.bs[:, 0:NC], T.xt[:]).then_inc(s.qz_x, 1)
-    if first:
-        quant_w(0); quant_w(1); act_v(1); quant_w(2); quant_w(3); act_v(3)
-    else:
-        for i in range(G):
-            quant_w(i)
+    for p, (a, b) in enumerate(cuts):
+        V.wait_ge(s["ld_w%d" % p], 16)
+        for k in range(a, b):
+            V.quantize_mx(T.bq[:, wcol(k)], T.bs[:, wcol(k)], T.wt[:, TW * k:TW * (k + 1)]).then_inc(s["qz_w%d" % k], 1)
+    if home and not first:
         quant_v()
-        act_v(1); act_v(3)
+    on_vector = (G - 1,) if first else tuple(range(1, G, 2))
+    for i in on_vector:
+        V.wait_ge(s["mm%d" % i], 1)
+        V.tensor_scalar(T.h[:, i:TW:4], zbank(i), 0.0, CF, AluOpType.max, AluOpType.mult).then_inc(s.act, 1)
     V.wait_ge(s.act, G)
     V.quantize_mx(T.qo[:], T.qos[:], T.h[:]).then_inc(s.qz_q, 1)
-    if first:
+    if first or not home:
         quant_v()
 
-    for i in (0, 2):
-        SC.wait_ge(s["mm%d" % i], 1)
-        SC.activation(T.h[:, i:TW:4], zbank(i), ActivationFunctionType.Relu, scale=CF).then_inc(s.act, 1)
+    for i in range(G):
+        if i not in on_vector:
+            SC.wait_ge(s["mm%d" % i], 1)
+            SC.activation(T.h[:, i:TW:4], zbank(i), ActivationFunctionType.Relu, scale=CF).then_inc(s.act, 1)
 
     def mm(i, t, rhs, rhs_s, start, stop):
         k = 2 * i + t
@@ -236,15 +281,15 @@ def rank_program(g, core, T, topo):
         if home:
             TE.wait_ge(s.qz_x, 1)
         else:
-            hp = _pair(cores, topo, cores[lay], core)
+            frm = _ways(cores, topo, cores[lay], core)
         for i in range(G):
             if home:
                 TE.wait_ge(s["qz_w%d" % (2 * i)], 1)
                 TE.wait_ge(s["qz_w%d" % (2 * i + 1)], 1)
             else:
-                TE.wait_ge(s["rb%d" % i], 2 * len(_engines(topo.mask(hp[i % 2] if hp else cores[lay], core))))
+                TE.wait_ge(s["rb%d" % i], 2 * len(_engines(topo.mask(frm[i] if frm else cores[lay], core))))
             mm(i, 1, Wq[:, 0:NC], Ws[:, 0:NC], True, False)
-        TE.wait_ge(s.arr, _q_count(cores, topo, cores[host[lay - 1]], core))
+        TE.wait_ge(s.arr, _q_count(cores, topo, host, cores[host[lay - 1]], core))
         for i in range(G):
             mm(i, 0, T.qin[:], T.qins[:], False, True).then_inc(s["mm%d" % i], 1)
     TE.wait_ge(s.qz_v, 1)
@@ -254,22 +299,9 @@ def rank_program(g, core, T, topo):
     elif lay == rank + 1:
         yq, ys = T.qin, T.qins
     else:
-        TE.wait_ge(s.yarr, _q_count(cores, topo, cores[host[rank]], core))
+        TE.wait_ge(s.yarr, _q_count(cores, topo, host, cores[host[rank]], core))
         yq, ys = T.qy, T.qys
     TE.matmul_mx(T.yp[:, 0:NC], T.vq[:], T.vs[:], yq[:], ys[:], True, True).then_inc(s.mm_y, 1)
-
-    if not home:
-        to = cores[host[rank]]
-        hp = _pair(cores, topo, core, to)
-        g.wait_ge(s.qz_x, 1)
-        for j in range(G):
-            g.wait_ge(s["qz_w%d" % (2 * j)], 1)
-            g.wait_ge(s["qz_w%d" % (2 * j + 1)], 1)
-            c = _piece(j)
-            d, sem = (hp[j % 2], s["hb%d" % j]) if hp else (to, s["rb%d" % j])
-            e = _engines(topo.mask(core, d))
-            write(d, T.rq[:, c].bitcast(dt.uint8), T.bq[:, c].bitcast(dt.uint8), sem, e)
-            write(d, T.rs[:, c], T.bs[:, c], sem, e)
 
     if qdst[lay]:
         g.wait_ge(s.qz_q, 1)
@@ -278,19 +310,22 @@ def rank_program(g, core, T, topo):
             hp = _pair(cores, topo, core, dst)
             if hp is None:
                 oc, os_, sem = land(kind)
-                ec, es = _q_engines(topo, core, dst, dst)
+                ec, es = _q_engines(topo, core, dst, dst, not home)
                 write(dst, oc[:].bitcast(dt.uint8), T.qo[:].bitcast(dt.uint8), sem, ec)
                 write(dst, os_[:], T.qos[:], sem, es)
             elif not handed:
-                ec, es = _q_engines(topo, core, hp[0], hp[1])
+                ec, es = _q_engines(topo, core, hp[0], hp[1], not home)
                 write(hp[0], T.qin[:].bitcast(dt.uint8), T.qo[:].bitcast(dt.uint8), s.arr, ec)
                 write(hp[1], T.qins[:], T.qos[:], s.arr, es)
                 handed = True
-    if n_sent[0]:
-        g.wait_ge(s.sent, n_sent[0])
+    for name in ("psent", "sent"):
+        if left[name]:
+            g.wait_ge(s[name], left[name])
 
     SC.wait_ge(s.mm_y, 1)
     SC.activation(T.yb[:], T.yp[:, 0:NC], ActivationFunctionType.Copy).then_inc(s.ycp, 1)
     SY.wait_ge(s.ycp, 1)
+    if left["sent"]:
+        SY.wait_ge(s.sent, left["sent"])
     SY.dma_start(T.y[:], T.yb[:]).then_inc(s.stored, 16)
     SY.wait_ge(s.stored, 16)

import numpy as np
from concourse.mybir import dt, AluOpType, ActivationFunctionType

NC, G = 128, 4
TW = 4 * NC
NT = 1 + 2 * G
CF = float(np.float32(0.0133))
SIM_CORES = 256

SCRATCH = {
    "st": ("sbuf", [128, TW], "bfloat16"),
    "xt": ("sbuf", [128, TW], "bfloat16"),
    "wt": ("sbuf", [128, 2 * G * TW], "bfloat16"),
    "vt": ("sbuf", [128, TW], "bfloat16"),
    "sq": ("sbuf", [128, NC], "float8_e4m3fn_x4"), "ss": ("sbuf", [128, NC], "uint8"),
    "bq": ("sbuf", [128, NT * NC], "float8_e4m3fn_x4"), "bs": ("sbuf", [128, NT * NC], "uint8"),
    "rq": ("sbuf", [128, NT * NC], "float8_e4m3fn_x4"), "rs": ("sbuf", [128, NT * NC], "uint8"),
    "vq": ("sbuf", [128, NC], "float8_e4m3fn_x4"), "vs": ("sbuf", [128, NC], "uint8"),
    "qin": ("sbuf", [128, NC], "float8_e4m3fn_x4"), "qins": ("sbuf", [128, NC], "uint8"),
    "qy": ("sbuf", [128, NC], "float8_e4m3fn_x4"), "qys": ("sbuf", [128, NC], "uint8"),
    "h": ("sbuf", [128, TW], "bfloat16"),
    "qo": ("sbuf", [128, NC], "float8_e4m3fn_x4"), "qos": ("sbuf", [128, NC], "uint8"),
    "yb": ("sbuf", [128, NC], "float32"),
    "z": ("psum", [128, 512 * G], "float32"),
    "yp": ("psum", [128, 512], "float32"),
}
SEMAPHORES = (["ld_s", "ld_x", "ld_v"] + ["ld_w%d" % i for i in range(G)]
              + ["qz_s", "qz_x", "qz_v", "qz_q"] + ["qz_w%d" % k for k in range(2 * G)]
              + ["mm%d" % i for i in range(G)] + ["mm_y", "act", "ycp", "stored", "arr", "yarr", "sent", "psent"]
              + ["hb%d" % i for i in range(G)] + ["rb%d" % i for i in range(G)])

_CACHE = {}


def _perms(items):
    if not items:
        return [()]
    out = []
    for i, a in enumerate(items):
        for rest in _perms(items[:i] + items[i + 1:]):
            out.append((a,) + rest)
    return out


def _same_chip(topo, a, b):
    return topo.host(a) == topo.host(b) and topo.chip(a) == topo.chip(b)


def _pair(cores, topo, src, dst):
    if topo.may_write(src, dst):
        return None
    near = [c for c in range(SIM_CORES) if c not in cores and _same_chip(topo, c, src)
            and topo.may_write(src, c) and topo.may_write(c, dst)]
    near.sort(key=lambda c: (topo.die(c) != topo.die(src), c))
    return near[0], near[1]


def _ways(cores, topo, src, dst):
    key = ("ways", src, dst)
    if key not in _CACHE:
        near = _pair(cores, topo, src, dst)
        if near is None:
            _CACHE[key] = None
        else:
            far = [c for c in range(SIM_CORES) if c not in cores and topo.mates(c, dst)
                   and topo.may_write(src, c) and topo.may_write(c, dst)]
            far.sort(key=lambda c: (topo.die(c) != topo.die(src), c))
            _CACHE[key] = tuple((far if j % 2 == 0 else near)[(j // 2) % 2] for j in range(G))
    return _CACHE[key]


def _plan(cores, topo):
    if "plan" in _CACHE:
        return _CACHE["plan"]
    n = len(cores)
    best = None
    for mid in _perms(tuple(range(1, n - 1))):
        h = (0,) + mid + (n - 1,)
        key = (sum(not topo.may_write(cores[h[l]], cores[h[l + 1]]) for l in range(n - 1)),
               sum(h[l] != l for l in range(n)),
               sum(h[l] != l and h[l + 1] != l for l in range(n - 1)),
               sum(topo.die(cores[h[l]]) != topo.die(cores[h[l + 1]]) for l in range(n - 1)), h)
        if best is None or key < best:
            best = key
    host = best[-1]
    qdst = []
    for l in range(n):
        d = []
        if l < n - 1:
            d.append((cores[host[l + 1]], "c"))
            if host[l] != l and host[l + 1] != l:
                d.append((cores[l], "y"))
        qdst.append(d)
    jobs = {}
    for l in range(n):
        if host[l] != l:
            src, dst = cores[l], cores[host[l]]
            via = _ways(cores, topo, src, dst)
            if via:
                for j in range(G):
                    jobs.setdefault(via[j], []).append(("b", j, src, dst))
    for l in range(n):
        src = cores[host[l]]
        via = [(d, k) for d, k in qdst[l] if not topo.may_write(src, d)]
        if via:
            hp = _pair(cores, topo, src, via[0][0])
            jobs.setdefault(hp[0], []).append(("q", 0, src, via))
            jobs.setdefault(hp[1], []).append(("q", 1, src, via))
    _CACHE["plan"] = (host, qdst, jobs)
    return _CACHE["plan"]


def _engines(mask):
    return [b for b in range(mask.bit_length()) if (mask >> b) & 1]


def _bits(engines):
    m = 0
    for b in engines:
        m |= 1 << b
    return m


def _b_engines(cores, topo, src, dst, j):
    via = _ways(cores, topo, src, dst)
    if via is None:
        return _engines(topo.mask(src, dst))
    e = _engines(topo.mask(src, via[j]))
    if _same_chip(topo, src, via[j]):
        away = [b for c in via if not _same_chip(topo, src, c) for b in _engines(topo.mask(src, c))]
        rest = [b for b in e if b not in away]
        return rest or e
    return e


def _q_engines(topo, src, dst_c, dst_s, sent_before):
    mc, ms = _engines(topo.mask(src, dst_c)), _engines(topo.mask(src, dst_s))
    if _same_chip(topo, src, dst_c) and not sent_before:
        return mc[0::2], ms[1::2]
    return mc, ms


def _away(cores, host, c):
    r = cores.index(c)
    return host[r] != r


def _q_count(cores, topo, host, src, dst):
    hp = _pair(cores, topo, src, dst)
    if hp is None:
        ec, es = _q_engines(topo, src, dst, dst, _away(cores, host, src))
        return len(ec) + len(es)
    return len(_engines(topo.mask(hp[0], dst))) + len(_engines(topo.mask(hp[1], dst)))


def _piece(j):
    return slice(0 if j == 0 else NC * (1 + 2 * j), NC * (3 + 2 * j))


def rank_program(g, core, T, topo):
    cores = list(T.cores)
    host, qdst, jobs = _plan(cores, topo)
    rank = T.rank_of(core)
    s = T.sem
    left = {"sent": 0, "psent": 0}

    def write(dst, out_ap, in_ap, sem, engines, lsem="sent"):
        rid, pid = topo.addr(dst, core)
        g.remote_dma(out_ap, in_ap, sem, s[lsem], pid, rid, _bits(engines))
        left[lsem] += len(engines)

    def land(kind):
        return (T.qin, T.qins, s.arr) if kind == "c" else (T.qy, T.qys, s.yarr)

    if rank is None:
        for what, j, src, to in jobs.get(core, []):
            if what == "b":
                c = _piece(j)
                g.wait_ge(s["hb%d" % j], 2 * len(_b_engines(cores, topo, src, to, j)))
                e = _engines(topo.mask(core, to))
                write(to, T.rq[:, c].bitcast(dt.uint8), T.rq[:, c].bitcast(dt.uint8), s["rb%d" % j], e)
                write(to, T.rs[:, c], T.rs[:, c], s["rb%d" % j], e)
            else:
                hp = _pair(cores, topo, src, to[0][0])
                g.wait_ge(s.arr, len(_q_engines(topo, src, hp[0], hp[1], _away(cores, host, src))[j]))
                for dst, kind in to:
                    oc, os_, sem = land(kind)
                    e = _engines(topo.mask(core, dst))
                    if j == 0:
                        write(dst, oc[:].bitcast(dt.uint8), T.qin[:].bitcast(dt.uint8), sem, e)
                    else:
                        write(dst, os_[:], T.qins[:], sem, e)
        if left["sent"]:
            g.wait_ge(s.sent, left["sent"])
        return

    lay = host.index(rank)
    home = lay == rank
    first = lay == 0
    TE, V, SC, SY = g.tensor, g.vector, g.scalar, g.sync
    Wq, Ws = (T.bq, T.bs) if home else (T.rq, T.rs)

    if first:
        cuts = ((0, G), (G, 2 * G - 1), (2 * G - 1, 2 * G))
    else:
        cuts = tuple((2 * i, 2 * i + 2) for i in range(G))
    loads = []
    if first:
        loads.append((T.st[:], T.s[:], s.ld_s))
    loads.append((T.xt[:], T.x[:], s.ld_x))
    for p, (a, b) in enumerate(cuts):
        loads.append((T.wt[:, TW * a:TW * b], T.w[:, TW * a:TW * b], s["ld_w%d" % p]))
    if home:
        loads.append((T.vt[:], T.v[:], s.ld_v))
    for k, (o, i_, sem) in enumerate(loads):
        (SY if k % 2 == 0 else SC).dma_start(o, i_).then_inc(sem, 16)

    def wcol(k):
        return slice(NC * (k + 1), NC * (k + 2))

    def zbank(i):
        return T.z[:, 512 * i:512 * i + NC]

    if not home:
        to = cores[host[rank]]
        via = _ways(cores, topo, core, to)
        g.wait_ge(s.qz_x, 1)
        for j in range(G):
            g.wait_ge(s["qz_w%d" % (2 * j)], 1)
            g.wait_ge(s["qz_w%d" % (2 * j + 1)], 1)
            c = _piece(j)
            d, sem = (via[j], s["hb%d" % j]) if via else (to, s["rb%d" % j])
            e = _b_engines(cores, topo, core, to, j)
            write(d, T.rq[:, c].bitcast(dt.uint8), T.bq[:, c].bitcast(dt.uint8), sem, e, "psent")
            write(d, T.rs[:, c], T.bs[:, c], sem, e, "psent")
        SY.wait_ge(s.psent, left["psent"])
        SY.dma_start(T.vt[:], T.v[:]).then_inc(s.ld_v, 16)

    def quant_v():
        V.wait_ge(s.ld_v, 16)
        V.quantize_mx(T.vq[:], T.vs[:], T.vt[:]).then_inc(s.qz_v, 1)

    if first:
        V.wait_ge(s.ld_s, 16)
        V.quantize_mx(T.sq[:], T.ss[:], T.st[:]).then_inc(s.qz_s, 1)
    V.wait_ge(s.ld_x, 16)
    V.quantize_mx(T.bq[:, 0:NC], T.bs[:, 0:NC], T.xt[:]).then_inc(s.qz_x, 1)
    for p, (a, b) in enumerate(cuts):
        V.wait_ge(s["ld_w%d" % p], 16)
        for k in range(a, b):
            V.quantize_mx(T.bq[:, wcol(k)], T.bs[:, wcol(k)], T.wt[:, TW * k:TW * (k + 1)]).then_inc(s["qz_w%d" % k], 1)
    if home and not first:
        quant_v()
    on_vector = (G - 1,) if first else tuple(range(1, G, 2))
    for i in on_vector:
        V.wait_ge(s["mm%d" % i], 1)
        V.tensor_scalar(T.h[:, i:TW:4], zbank(i), 0.0, CF, AluOpType.max, AluOpType.mult).then_inc(s.act, 1)
    V.wait_ge(s.act, G)
    V.quantize_mx(T.qo[:], T.qos[:], T.h[:]).then_inc(s.qz_q, 1)
    if first or not home:
        quant_v()

    for i in range(G):
        if i not in on_vector:
            SC.wait_ge(s["mm%d" % i], 1)
            SC.activation(T.h[:, i:TW:4], zbank(i), ActivationFunctionType.Relu, scale=CF).then_inc(s.act, 1)

    def mm(i, t, rhs, rhs_s, start, stop):
        k = 2 * i + t
        return TE.matmul_mx(zbank(i), Wq[:, wcol(k)], Ws[:, wcol(k)], rhs, rhs_s, start, stop)

    if first:
        TE.wait_ge(s.qz_x, 1)
        TE.wait_ge(s.qz_s, 1)
        for i in range(G):
            TE.wait_ge(s["qz_w%d" % (2 * i)], 1)
            mm(i, 0, T.sq[:], T.ss[:], True, False)
            TE.wait_ge(s["qz_w%d" % (2 * i + 1)], 1)
            mm(i, 1, Wq[:, 0:NC], Ws[:, 0:NC], False, True).then_inc(s["mm%d" % i], 1)
    else:
        if home:
            TE.wait_ge(s.qz_x, 1)
        else:
            frm = _ways(cores, topo, cores[lay], core)
        for i in range(G):
            if home:
                TE.wait_ge(s["qz_w%d" % (2 * i)], 1)
                TE.wait_ge(s["qz_w%d" % (2 * i + 1)], 1)
            else:
                TE.wait_ge(s["rb%d" % i], 2 * len(_engines(topo.mask(frm[i] if frm else cores[lay], core))))
            mm(i, 1, Wq[:, 0:NC], Ws[:, 0:NC], True, False)
        TE.wait_ge(s.arr, _q_count(cores, topo, host, cores[host[lay - 1]], core))
        for i in range(G):
            mm(i, 0, T.qin[:], T.qins[:], False, True).then_inc(s["mm%d" % i], 1)
    TE.wait_ge(s.qz_v, 1)
    if home:
        TE.wait_ge(s.qz_q, 1)
        yq, ys = T.qo, T.qos
    elif lay == rank + 1:
        yq, ys = T.qin, T.qins
    else:
        TE.wait_ge(s.yarr, _q_count(cores, topo, host, cores[host[rank]], core))
        yq, ys = T.qy, T.qys
    TE.matmul_mx(T.yp[:, 0:NC], T.vq[:], T.vs[:], yq[:], ys[:], True, True).then_inc(s.mm_y, 1)

    if qdst[lay]:
        g.wait_ge(s.qz_q, 1)
        handed = False
        for dst, kind in qdst[lay]:
            hp = _pair(cores, topo, core, dst)
            if hp is None:
                oc, os_, sem = land(kind)
                ec, es = _q_engines(topo, core, dst, dst, not home)
                write(dst, oc[:].bitcast(dt.uint8), T.qo[:].bitcast(dt.uint8), sem, ec)
                write(dst, os_[:], T.qos[:], sem, es)
            elif not handed:
                ec, es = _q_engines(topo, core, hp[0], hp[1], not home)
                write(hp[0], T.qin[:].bitcast(dt.uint8), T.qo[:].bitcast(dt.uint8), s.arr, ec)
                write(hp[1], T.qins[:], T.qos[:], s.arr, es)
                handed = True
    for name in ("psent", "sent"):
        if left[name]:
            g.wait_ge(s[name], left[name])

    SC.wait_ge(s.mm_y, 1)
    SC.activation(T.yb[:], T.yp[:, 0:NC], ActivationFunctionType.Copy).then_inc(s.ycp, 1)
    SY.wait_ge(s.ycp, 1)
    if left["sent"]:
        SY.wait_ge(s.sent, left["sent"])
    SY.dma_start(T.y[:], T.yb[:]).then_inc(s.stored, 16)
    SY.wait_ge(s.stored, 16)
